import numpy as np
import ml_dtypes


def mxq(x, axis, fmt="e4m3"):
    dtype, down = {"e4m3": (ml_dtypes.float8_e4m3fn, 7), "e5m2": (ml_dtypes.float8_e5m2, 14)}[fmt]
    v = np.moveaxis(np.asarray(x, np.float32).astype(ml_dtypes.bfloat16).astype(np.float64), axis, -1)
    blocks = v.reshape(v.shape[:-1] + (-1, 32))
    amax = np.abs(blocks).max(-1, keepdims=True)
    byte = np.maximum(np.where(amax > 0, np.frexp(amax)[1] - 1 + 127, 0) - down, 1)
    scale = np.exp2(byte - 127.0)
    codes = (blocks / scale).astype(np.float32).astype(dtype).astype(np.float64)
    return np.moveaxis((codes * scale).reshape(v.shape), -1, axis)


WIDE = False


def mx_kscale(k):
    if not WIDE:
        return np.ones(k)
    levels = np.array([10, -10, 5, -5, 0])
    if k % 512:
        return np.exp2(np.random.permutation(np.resize(levels, k // 32))).repeat(32)
    a = np.empty((k // 512, 16))
    for p in range(k // 512):
        a[p, :8] = np.random.permutation(np.resize(levels, 8))
        for g in range(8):
            far = levels[np.abs(levels - a[p, g]) >= 10]
            a[p, g + 8] = far[np.random.randint(len(far))]
    return np.exp2(a.ravel()).repeat(32)


def f64(x):
    return np.asarray(x).astype(np.float64)


def striped(idx):
    return np.tile(idx.reshape(-1, 16).T, (8, 1)).astype(np.uint16)


def unstriped(offs):
    return offs[:16].T.reshape(-1).astype(np.int64)


def pack_weight(w):
    k, n = w.shape
    w = f64(np.asarray(w, np.float32).astype(ml_dtypes.bfloat16)).reshape(k // 32, 32, n)
    amax = np.abs(w).max(1)
    byte = np.clip(np.where(amax > 0, np.frexp(amax)[1] - 1 + 127 - 7, 1), 1, 254)
    scaled = (w * np.exp2(127.0 - byte)[:, None, :]).reshape(k, n).astype(np.float32)
    words = np.ascontiguousarray(scaled.reshape(k // 512, 128, 4, n).transpose(0, 1, 3, 2)).astype(ml_dtypes.float8_e4m3fn).view(np.uint8)
    return words, np.ascontiguousarray(byte.astype(np.uint8).reshape(k // 512, 16, n))


def unpack_weight(words, scales):
    g, p, n, _ = words.shape
    vals = np.ascontiguousarray(words).view(ml_dtypes.float8_e4m3fn).astype(np.float64) * np.repeat(np.exp2(scales.astype(np.float64) - 127.0), 8, axis=1)[..., None]
    return vals.transpose(0, 1, 3, 2).reshape(g * 512, n)


K, T, S, N, H, U = 512, 1024, 512, 128, 512, 1024


def setup_inputs():
    n = np.random.standard_normal
    s = mx_kscale(K)[:, None]
    u = mx_kscale(H)
    packed_xT = pack_weight(n((K, T)) * s)
    return {
        "x_words": packed_xT[0],
        "x_scales": packed_xT[1],
        "w1": (n((K, H)) / np.sqrt(K) / s).astype(np.float32),
        "wa": (np.random.uniform(0.1, 0.45, (H, U))).astype(np.float32),
        "wb": (np.random.uniform(0.1, 0.45, (H, U))).astype(np.float32),
        "unit": (np.random.uniform(0.6, 1.4, (H, 1)) * u[:, None]).astype(np.float32),
        "w2": (n((H, N)) / np.sqrt(H) / u[:, None]).astype(np.float32),
        "offs": striped(np.random.permutation(T)[:S]),
        "va": striped(np.random.permutation(np.concatenate([np.arange(S), np.random.randint(0, S, U - S)]))),
        "vb": striped(np.random.permutation(np.concatenate([np.arange(S), np.random.randint(0, S, U - S)]))),
        "vc": striped(np.random.permutation(np.concatenate([np.arange(S), np.random.randint(0, S, U - S)]))),
    }


def reference(x_words, x_scales, w1, wa, wb, unit, w2, offs, va, vb, vc):
    xq = unpack_weight(x_words, x_scales)[:, unstriped(offs)]
    y = mxq(f64(w1), 0, "e4m3").T @ xq
    ya = y[:, unstriped(va)]
    yb = y[:, unstriped(vb)]
    yvc = y[:, unstriped(vc)]
    fine = f64(wa) * ya + f64(wb) * yb + yvc * (-1.0 * (f64(wa) + f64(wb)) + 1.0)
    hid = f64(unit) * fine
    return mxq(f64(w2), 0, "e4m3").T @ mxq(hid, 0, "e4m3")

@@ -1,0 +1,221 @@
+from contextlib import ExitStack
+
+import concourse.mybir as mybir
+from concourse.masks import make_identity
+
+F32 = mybir.dt.float32
+BF16 = mybir.dt.bfloat16
+I32 = mybir.dt.int32
+U32 = mybir.dt.uint32
+U16 = mybir.dt.uint16
+U8 = mybir.dt.uint8
+FP8X4 = mybir.dt.float8_e4m3fn_x4
+ALU = mybir.AluOpType
+COPY = mybir.ActivationFunctionType.Copy
+
+K, T, S, N, H, U = 512, 1024, 512, 128, 512, 1024
+P = 128
+PACK = 4
+BLOCKS = H // P
+BANK = 512
+WIDTHS = ((512, 512), (1024,), (1024,), (256, 256, 256, 128, 128))
+VECTOR_B = (4, 5, 6, 7, 8)
+WINDOW = max(max(w) for w in WIDTHS) + 16
+
+FLOPS = 2 * K * H * S + 2 * H * N * U
+
+
+def tile_picked_ybaryin_lin_p_kernel(
+    tc, x_words, x_scales, w1, wa, wb, unit, w2, offs, va, vb, vc, out
+):
+    nc = tc.nc
+    with ExitStack() as ctx:
+        held = ctx.enter_context(tc.tile_pool(name="held", bufs=1))
+        ring = ctx.enter_context(tc.tile_pool(name="ring", bufs=2))
+        psum = ctx.enter_context(tc.psum_pool(name="psum", bufs=1))
+
+        steps = [
+            (u, sum(WIDTHS[u][:n]), width) for u in range(BLOCKS) for n, width in enumerate(WIDTHS[u])
+        ]
+
+        table_scales = held.tile([P, T], U8, name="table_scales")
+        nc.gpsimd.memset(table_scales[:].bitcast(I32), 0)
+        offs_sb = held.tile([P, S // 16], U16, name="offs_sb")
+        nc.sync.dma_start(offs_sb[:], offs)
+        w1_rows = w1.rearrange("(p j) c -> p j c", j=PACK)
+        w1_raw = [held.tile([P, PACK, P], F32, name=f"w1_raw{u}") for u in range(BLOCKS)]
+
+        def load_w1(u):
+            nc.sync.dma_start(w1_raw[u][:], w1_rows[:, :, u * P : (u + 1) * P])
+
+        load_w1(0)
+        for r in range(4):
+            nc.sync.dma_start(
+                table_scales[r:P:32, :].bitcast(I32), x_scales[0].bitcast(I32)[r:16:4, :]
+            )
+        table_words = held.tile([P, T], U32, name="table_words")
+        nc.sync.dma_start(
+            table_words[:].bitcast(I32), x_words[0].rearrange("p n t -> p (n t)").bitcast(I32)
+        )
+        lists = {name: held.tile([P, U // 16], U16, name=f"list_{name}") for name in "abc"}
+        unit_sb = held.tile([P, BLOCKS], F32, name="unit_sb")
+        w2_raw = held.tile([P, PACK, N], F32, name="w2_raw")
+        weights = {}
+
+        def load_weights(u, first, width):
+            for name, src in (("a", wa), ("b", wb)):
+                loaded = held.tile([P, width], F32, name=f"w{name}{u}_{first}")
+                nc.sync.dma_start(loaded[:], src[u * P : (u + 1) * P, first : first + width])
+                for i, (block, start, size) in enumerate(steps):
+                    if block == u and first <= start < first + width:
+                        weights[i, name] = loaded[:, start - first : start - first + size]
+
+        nc.sync.dma_start(lists["c"][:], vc)
+        nc.sync.dma_start(lists["a"][:], va)
+        with nc.allow_non_contiguous_dma(reason="one factor a partition"):
+            nc.sync.dma_start(unit_sb[:], unit.rearrange("(u p) o -> p (u o)", p=P))
+        load_w1(1)
+        load_weights(0, 0, U // 2)
+        nc.sync.dma_start(lists["b"][:], vb)
+        load_weights(0, U // 2, U // 2)
+        load_w1(2)
+        load_weights(1, 0, U)
+        load_w1(3)
+        load_weights(2, 0, U)
+        nc.sync.dma_start(w2_raw[:], w2.rearrange("(p j) m -> p j m", j=PACK))
+        load_weights(3, 0, U)
+
+        ident = held.tile([P, P], F32, name="ident")
+        windows = [held.tile([P, WINDOW], F32, name=f"window{u}") for u in range(BLOCKS)]
+        for u in range(BLOCKS):
+            nc.gpsimd.memset(windows[u][:, S:], 0.0)
+        make_identity(nc, ident[:])
+
+        def quantise_weight(raw, name, on_scalar):
+            grouped = held.tile([P, P, PACK], BF16, name=f"{name}_bf", align_bytes=64)
+            if on_scalar:
+                nc.scalar.activation(grouped[:], raw[:].rearrange("p j c -> p c j"), COPY)
+            else:
+                nc.vector.tensor_copy(grouped[:], raw[:].rearrange("p j c -> p c j"))
+            codes = held.tile([P, P], U32, name=f"{name}_codes", align_bytes=64)
+            scales = held.tile([P, P], U8, name=f"{name}_scales", align_bytes=64)
+            nc.vector.quantize_mx(
+                out=codes[:].bitcast(FP8X4), scales=scales[:], in_=grouped[:].rearrange("p c j -> p (c j)")
+            )
+            return codes, scales
+
+        x_codes = held.tile([P, S], U32, name="x_codes", align_bytes=64)
+        x_bytes = held.tile([P, S], U8, name="x_bytes", align_bytes=64)
+        nc.vector.tensor_copy(x_bytes[:], table_scales[:].indirect(offs_sb[:]))
+        nc.vector.tensor_copy(x_codes[:], table_words[:].indirect(offs_sb[:]))
+
+        def coarse_block(u):
+            codes, scales = quantise_weight(w1_raw[u], f"w1_{u}", u < 2)
+            y = psum.tile([P, S], F32, name="y", tag="mx", bufs=2)
+            nc.tensor.matmul_mx(
+                out=y[:], lhsT=codes[:].bitcast(FP8X4), lhsT_scale=scales[:],
+                rhs=x_codes[:].bitcast(FP8X4), rhs_scale=x_bytes[:], start=True, stop=True,
+            )
+            nc.scalar.activation(windows[u][:, :S], y[:], COPY, scale=unit_sb[:, u : u + 1])
+
+        def corners(i, name):
+            u, first, width = steps[i]
+            return windows[u][:].indirect(lists[name][:, first // 16 : (first + width) // 16])
+
+        fetched = {}
+
+        def scalar_fetch(i):
+            width = steps[i][2]
+            for name in ("c",) if i in VECTOR_B else ("c", "b"):
+                fetched[i, name] = ring.tile([P, width], F32, name=f"fetched_{name}")
+                nc.scalar.activation(fetched[i, name][:], corners(i, name), COPY)
+
+        sums = {}
+
+        def terms(i):
+            u, first, width = steps[i]
+            minus_sum = ring.tile([P, width], F32, name="minus_sum")
+            nc.vector.scalar_tensor_tensor(
+                minus_sum[:], weights[i, "a"], -1.0, weights[i, "b"], ALU.mult, ALU.subtract
+            )
+            term_a = ring.tile([P, width], F32, name="term_a")
+            nc.vector.tensor_tensor(term_a[:], corners(i, "a"), weights[i, "a"], ALU.mult)
+            term_c = ring.tile([P, width], F32, name="term_c")
+            term_b = ring.tile([P, width], F32, name="term_b")
+            if i in VECTOR_B:
+                nc.vector.tensor_tensor(term_b[:], corners(i, "b"), weights[i, "b"], ALU.mult)
+            nc.vector.scalar_tensor_tensor(
+                term_c[:], minus_sum[:], 1.0, fetched[i, "c"][:], ALU.add, ALU.mult
+            )
+            if i not in VECTOR_B:
+                nc.vector.tensor_tensor(term_b[:], fetched[i, "b"][:], weights[i, "b"], ALU.mult)
+            three = (term_a, term_b, term_c) if i in VECTOR_B else (term_a, term_c, term_b)
+            parts = [(at, min(BANK, width - at)) for at in range(0, width, BANK)]
+            sums[i] = [
+                (at, size, psum.tile([P, size // P, P], F32, name="sums", bufs=4)) for at, size in parts
+            ]
+            for n, term in enumerate(three):
+                for at, size, bank in sums[i]:
+                    for c in range(size // P):
+                        nc.tensor.matmul(
+                            bank[:, c, :], lhsT=term[:, at + c * P : at + (c + 1) * P], rhs=ident[:],
+                            start=(n == 0 and c == 0), stop=(n == len(three) - 1 and c == size // P - 1),
+                            is_transpose=True,
+                        )
+
+        turned = held.tile([P, 2, U // P, P, 2], BF16, name="turned")
+        turned_words = turned[:].rearrange("r w c p e -> r (w c p e)").bitcast(F32)
+
+        def round_sums(i):
+            u, first, width = steps[i]
+            for at, size, bank in sums[i]:
+                nc.scalar.copy(
+                    turned[:, :, (first + at) // P : (first + at + size) // P, 32 * u : 32 * (u + 1), :],
+                    bank[:].rearrange("r c (q w e) -> r w c q e", w=2, e=2),
+                )
+
+        def decode(first, width, copy_words, copy_out):
+            grouped = ring.tile([P, width, PACK], BF16, name="hid_bf", align_bytes=64)
+            back = psum.tile([P, 2, width], F32, name="back", bufs=2)
+            for w in range(2):
+                for c in range(width // P):
+                    at = w * U + first + c * P
+                    nc.tensor.transpose(back[:, w, c * P : (c + 1) * P], turned_words[:, at : at + P], ident[:])
+            copy_words(
+                grouped[:].rearrange("p r j -> p (r j)").bitcast(F32).rearrange("p (r w) -> p r w", w=2),
+                back[:].rearrange("p w r -> p r w"),
+            )
+            codes = ring.tile([P, width], U32, name="hid_codes", align_bytes=64)
+            scales = ring.tile([P, width], U8, name="hid_scales", align_bytes=64)
+            nc.vector.quantize_mx(
+                out=codes[:].bitcast(FP8X4), scales=scales[:], in_=grouped[:].rearrange("p r j -> p (r j)")
+            )
+            result = psum.tile([P, width], F32, name="result", tag="mx", bufs=2)
+            nc.tensor.matmul_mx(
+                out=result[:], lhsT=w2_codes[:].bitcast(FP8X4), lhsT_scale=w2_scales[:],
+                rhs=codes[:].bitcast(FP8X4), rhs_scale=scales[:], start=True, stop=True,
+            )
+            staged = held.tile([P, width], F32, name=f"staged{first}")
+            copy_out(staged[:], result[:])
+            nc.sync.dma_start(out[:, first : first + width], staged[:])
+
+        def finish(i):
+            round_sums(i)
+            u, first, width = steps[i]
+            if u == BLOCKS - 1:
+                last = i == len(steps) - 1
+                decode(first, width, nc.vector.tensor_copy if last else nc.scalar.copy, nc.scalar.copy)
+
+        coarse_block(0)
+        scalar_fetch(0)
+        for i, (u, first, width) in enumerate(steps):
+            if first == 0 and u + 1 < BLOCKS:
+                coarse_block(u + 1)
+            if first == 0 and u + 1 == BLOCKS:
+                w2_codes, w2_scales = quantise_weight(w2_raw, "w2", False)
+            if i + 1 < len(steps):
+                scalar_fetch(i + 1)
+            terms(i)
+            if i > 0:
+                finish(i - 1)
+        finish(len(steps) - 1)

@@ -17,10 +17,12 @@ K, T, S, N, H, U = 512, 1024, 512, 128, 512, 1024
 P = 128
 PACK = 4
 BLOCKS = H // P
-BANK = 512
-WIDTHS = ((512, 512), (1024,), (1024,), (256, 256, 256, 128, 128))
-VECTOR_B = (4, 5, 6, 7, 8)
-WINDOW = max(max(w) for w in WIDTHS) + 16
+HALF = U // 2
+LAST = 128
+PIECE = 256
+WINDOW = S + 16
+VECTOR_B = (0, 6)
+X_PARTS = 2
 
 FLOPS = 2 * K * H * S + 2 * H * N * U
 
@@ -34,31 +36,30 @@ def tile_picked_ybaryin_lin_p_kernel(
         ring = ctx.enter_context(tc.tile_pool(name="ring", bufs=2))
         psum = ctx.enter_context(tc.psum_pool(name="psum", bufs=1))
 
-        steps = [
-            (u, sum(WIDTHS[u][:n]), width) for u in range(BLOCKS) for n, width in enumerate(WIDTHS[u])
-        ]
+        steps = [(0, 0, 512), (0, 512, 512), (1, 0, 512), (1, 512, 512), (2, 0, 512), (2, 512, 512), (3, 0, 256), (3, 256, 256), (3, 512, 256), (3, 768, 128), (3, 896, 128)]
+        fields = steps
 
         table_scales = held.tile([P, T], U8, name="table_scales")
         nc.gpsimd.memset(table_scales[:].bitcast(I32), 0)
         offs_sb = held.tile([P, S // 16], U16, name="offs_sb")
         nc.sync.dma_start(offs_sb[:], offs)
-        w1_rows = w1.rearrange("(p j) c -> p j c", j=PACK)
-        w1_raw = [held.tile([P, PACK, P], F32, name=f"w1_raw{u}") for u in range(BLOCKS)]
-
-        def load_w1(u):
-            nc.sync.dma_start(w1_raw[u][:], w1_rows[:, :, u * P : (u + 1) * P])
-
-        load_w1(0)
+        unit_first = held.tile([P, 1], F32, name="unit_first")
+        nc.scalar.dma_start(unit_first[:], unit[:P, :])
         for r in range(4):
-            nc.sync.dma_start(
-                table_scales[r:P:32, :].bitcast(I32), x_scales[0].bitcast(I32)[r:16:4, :]
-            )
+            queue = nc.scalar if r % 2 else nc.sync
+            queue.dma_start(table_scales[r:P:32, :].bitcast(I32), x_scales[0].bitcast(I32)[r:16:4, :])
         table_words = held.tile([P, T], U32, name="table_words")
         nc.sync.dma_start(
             table_words[:].bitcast(I32), x_words[0].rearrange("p n t -> p (n t)").bitcast(I32)
         )
+        w1_rows = w1.rearrange("(p j) c -> p j c", j=PACK)
+        w1_raw = [held.tile([P, PACK, P], F32, name=f"w1_raw{u}") for u in range(BLOCKS)]
+        nc.scalar.dma_start(w1_raw[0][:], w1_rows[:, :, :P])
         lists = {name: held.tile([P, U // 16], U16, name=f"list_{name}") for name in "abc"}
-        unit_sb = held.tile([P, BLOCKS], F32, name="unit_sb")
+        nc.sync.dma_start(lists["c"][:], vc)
+        nc.sync.dma_start(lists["a"][:], va)
+        unit_rest = held.tile([P, BLOCKS - 1], F32, name="unit_rest")
+        units = [unit_first[:]] + [unit_rest[:, u : u + 1] for u in range(BLOCKS - 1)]
         w2_raw = held.tile([P, PACK, N], F32, name="w2_raw")
         weights = {}
 
@@ -70,19 +71,26 @@ def tile_picked_ybaryin_lin_p_kernel(
                     if block == u and first <= start < first + width:
                         weights[i, name] = loaded[:, start - first : start - first + size]
 
-        nc.sync.dma_start(lists["c"][:], vc)
-        nc.sync.dma_start(lists["a"][:], va)
-        with nc.allow_non_contiguous_dma(reason="one factor a partition"):
-            nc.sync.dma_start(unit_sb[:], unit.rearrange("(u p) o -> p (u o)", p=P))
+        def load_w1(u):
+            nc.sync.dma_start(w1_raw[u][:], w1_rows[:, :, u * P : (u + 1) * P])
+
+        def load_unit():
+            with nc.allow_non_contiguous_dma(reason="one factor a partition"):
+                nc.sync.dma_start(unit_rest[:], unit[P:, :].rearrange("(u p) o -> p (u o)", p=P))
+
+        def load_w2():
+            nc.sync.dma_start(w2_raw[:], w2.rearrange("(p j) m -> p j m", j=PACK))
+
         load_w1(1)
-        load_weights(0, 0, U // 2)
+        load_weights(0, 0, HALF)
         nc.sync.dma_start(lists["b"][:], vb)
-        load_weights(0, U // 2, U // 2)
+        load_unit()
+        load_weights(0, HALF, HALF)
         load_w1(2)
-        load_weights(1, 0, U)
         load_w1(3)
+        load_weights(1, 0, U)
+        load_w2()
         load_weights(2, 0, U)
-        nc.sync.dma_start(w2_raw[:], w2.rearrange("(p j) m -> p j m", j=PACK))
         load_weights(3, 0, U)
 
         ident = held.tile([P, P], F32, name="ident")
@@ -107,72 +115,78 @@ def tile_picked_ybaryin_lin_p_kernel(
         x_codes = held.tile([P, S], U32, name="x_codes", align_bytes=64)
         x_bytes = held.tile([P, S], U8, name="x_bytes", align_bytes=64)
         nc.vector.tensor_copy(x_bytes[:], table_scales[:].indirect(offs_sb[:]))
-        nc.vector.tensor_copy(x_codes[:], table_words[:].indirect(offs_sb[:]))
+        x_width = S // X_PARTS
+        for at in range(0, S, x_width):
+            nc.vector.tensor_copy(
+                x_codes[:, at : at + x_width],
+                table_words[:].indirect(offs_sb[:, at // 16 : (at + x_width) // 16]),
+            )
 
         def coarse_block(u):
-            codes, scales = quantise_weight(w1_raw[u], f"w1_{u}", u < 2)
-            y = psum.tile([P, S], F32, name="y", tag="mx", bufs=2)
-            nc.tensor.matmul_mx(
-                out=y[:], lhsT=codes[:].bitcast(FP8X4), lhsT_scale=scales[:],
-                rhs=x_codes[:].bitcast(FP8X4), rhs_scale=x_bytes[:], start=True, stop=True,
-            )
-            nc.scalar.activation(windows[u][:, :S], y[:], COPY, scale=unit_sb[:, u : u + 1])
+            codes, scales = quantise_weight(w1_raw[u], f"w1_{u}", u in (0,))
+            width = x_width if u == 0 else S
+            for at in range(0, S, width):
+                y = psum.tile([P, width], F32, name="y", tag="mx", bufs=2)
+                nc.tensor.matmul_mx(
+                    out=y[:], lhsT=codes[:].bitcast(FP8X4), lhsT_scale=scales[:],
+                    rhs=x_codes[:, at : at + width].bitcast(FP8X4), rhs_scale=x_bytes[:, at : at + width],
+                    start=True, stop=True,
+                )
+                nc.scalar.activation(windows[u][:, at : at + width], y[:], COPY, scale=units[u])
 
-        def corners(i, name):
-            u, first, width = steps[i]
+        def corners(name, u, first, width):
             return windows[u][:].indirect(lists[name][:, first // 16 : (first + width) // 16])
 
-        fetched = {}
+        fetched, minus_sum = {}, {}
 
-        def scalar_fetch(i):
-            width = steps[i][2]
-            for name in ("c",) if i in VECTOR_B else ("c", "b"):
-                fetched[i, name] = ring.tile([P, width], F32, name=f"fetched_{name}")
-                nc.scalar.activation(fetched[i, name][:], corners(i, name), COPY)
+        def scalar_fetch(f):
+            u, first, width = steps[f]
+            for name in ("c",) if f in VECTOR_B else ("c", "b"):
+                fetched[f, name] = ring.tile([P, width], F32, name=f"fetched_{name}", bufs=2)
+                nc.scalar.activation(fetched[f, name][:], corners(name, u, first, width), COPY)
+
+        def add_weights(f):
+            minus_sum[f] = ring.tile([P, steps[f][2]], F32, name="minus_sum", bufs=2)
+            nc.vector.scalar_tensor_tensor(
+                minus_sum[f][:], weights[f, "a"], -1.0, weights[f, "b"], ALU.mult, ALU.subtract
+            )
 
         sums = {}
 
         def terms(i):
             u, first, width = steps[i]
-            minus_sum = ring.tile([P, width], F32, name="minus_sum")
-            nc.vector.scalar_tensor_tensor(
-                minus_sum[:], weights[i, "a"], -1.0, weights[i, "b"], ALU.mult, ALU.subtract
-            )
-            term_a = ring.tile([P, width], F32, name="term_a")
-            nc.vector.tensor_tensor(term_a[:], corners(i, "a"), weights[i, "a"], ALU.mult)
-            term_c = ring.tile([P, width], F32, name="term_c")
-            term_b = ring.tile([P, width], F32, name="term_b")
-            if i in VECTOR_B:
-                nc.vector.tensor_tensor(term_b[:], corners(i, "b"), weights[i, "b"], ALU.mult)
-            nc.vector.scalar_tensor_tensor(
-                term_c[:], minus_sum[:], 1.0, fetched[i, "c"][:], ALU.add, ALU.mult
-            )
-            if i not in VECTOR_B:
-                nc.vector.tensor_tensor(term_b[:], fetched[i, "b"][:], weights[i, "b"], ALU.mult)
-            three = (term_a, term_b, term_c) if i in VECTOR_B else (term_a, term_c, term_b)
-            parts = [(at, min(BANK, width - at)) for at in range(0, width, BANK)]
-            sums[i] = [
-                (at, size, psum.tile([P, size // P, P], F32, name="sums", bufs=4)) for at, size in parts
-            ]
-            for n, term in enumerate(three):
-                for at, size, bank in sums[i]:
-                    for c in range(size // P):
-                        nc.tensor.matmul(
-                            bank[:, c, :], lhsT=term[:, at + c * P : at + (c + 1) * P], rhs=ident[:],
-                            start=(n == 0 and c == 0), stop=(n == len(three) - 1 and c == size // P - 1),
-                            is_transpose=True,
-                        )
+            f = i
+            cols = slice(0, width)
+            term = {name: ring.tile([P, width], F32, name=f"term_{name}") for name in "abc"}
+            nc.vector.tensor_tensor(term["a"][:], corners("a", u, first, width), weights[f, "a"], ALU.mult)
+            corner_b = corners("b", u, first, width) if f in VECTOR_B else fetched[f, "b"][:, cols]
+            order = "abc" if f in VECTOR_B else "acb"
+            for name in order[1:]:
+                if name == "b":
+                    nc.vector.tensor_tensor(term["b"][:], corner_b, weights[f, "b"], ALU.mult)
+                else:
+                    nc.vector.scalar_tensor_tensor(
+                        term["c"][:], minus_sum[f][:, cols], 1.0, fetched[f, "c"][:, cols], ALU.add, ALU.mult
+                    )
+            chunks = width // P
+            sums[i] = psum.tile([P, chunks, P], F32, name="sums", bufs=4)
+            for name in order:
+                for c in range(chunks):
+                    nc.tensor.matmul(
+                        sums[i][:, c, :], lhsT=term[name][:, c * P : (c + 1) * P], rhs=ident[:],
+                        start=(name == order[0] and c == 0), stop=(name == order[-1] and c == chunks - 1),
+                        is_transpose=True,
+                    )
 
         turned = held.tile([P, 2, U // P, P, 2], BF16, name="turned")
         turned_words = turned[:].rearrange("r w c p e -> r (w c p e)").bitcast(F32)
 
         def round_sums(i):
             u, first, width = steps[i]
-            for at, size, bank in sums[i]:
-                nc.scalar.copy(
-                    turned[:, :, (first + at) // P : (first + at + size) // P, 32 * u : 32 * (u + 1), :],
-                    bank[:].rearrange("r c (q w e) -> r w c q e", w=2, e=2),
-                )
+            (nc.scalar.copy)(
+                turned[:, :, first // P : (first + width) // P, 32 * u : 32 * (u + 1), :],
+                sums[i][:].rearrange("r c (q w e) -> r w c q e", w=2, e=2),
+            )
 
         def decode(first, width, copy_words, copy_out):
             grouped = ring.tile([P, width, PACK], BF16, name="hid_bf", align_bytes=64)
@@ -202,20 +216,32 @@ def tile_picked_ybaryin_lin_p_kernel(
         def finish(i):
             round_sums(i)
             u, first, width = steps[i]
+            last = i == len(steps) - 1
             if u == BLOCKS - 1:
-                last = i == len(steps) - 1
-                decode(first, width, nc.vector.tensor_copy if last else nc.scalar.copy, nc.scalar.copy)
+                for at in range(first, first + width, PIECE):
+                    decode(
+                        at,
+                        min(PIECE, first + width - at),
+                        nc.vector.tensor_copy if last else nc.scalar.copy,
+                        nc.vector.tensor_copy if False else nc.scalar.copy,
+                    )
 
+        made = {0}
         coarse_block(0)
         scalar_fetch(0)
-        for i, (u, first, width) in enumerate(steps):
-            if first == 0 and u + 1 < BLOCKS:
-                coarse_block(u + 1)
-            if first == 0 and u + 1 == BLOCKS:
-                w2_codes, w2_scales = quantise_weight(w2_raw, "w2", False)
-            if i + 1 < len(steps):
+        add_weights(0)
+        for i in range(len(steps)):
+            ahead = steps[min(i + 2, len(steps) - 1)][0]
+            if ahead not in made:
+                made.add(ahead)
+                coarse_block(ahead)
+            if i == 4:
+                w2_codes, w2_scales = quantise_weight(w2_raw, "w2", True)
+            if i + 1 < len(fields):
                 scalar_fetch(i + 1)
             terms(i)
+            if i + 1 < len(fields):
+                add_weights(i + 1)
             if i > 0:
                 finish(i - 1)
         finish(len(steps) - 1)

@@ -16,13 +16,14 @@ COPY = mybir.ActivationFunctionType.Copy
 K, T, S, N, H, U = 512, 1024, 512, 128, 512, 1024
 P = 128
 PACK = 4
+PAIRS = PACK // 2
+LIST_ROWS = 16
+QUADRANT = 32
+SCALE_ROWS = 4
 BLOCKS = H // P
 HALF = U // 2
-LAST = 128
-PIECE = 256
-WINDOW = S + 16
-VECTOR_B = (0, 6)
-X_PARTS = 2
+LAST_WIDTHS = (256, 256, 256, 128, 128)
+SPARE = 16
 
 FLOPS = 2 * K * H * S + 2 * H * N * U
 
@@ -31,80 +32,77 @@ def tile_picked_ybaryin_lin_p_kernel(
     tc, x_words, x_scales, w1, wa, wb, unit, w2, offs, va, vb, vc, out
 ):
     nc = tc.nc
+    last_block = BLOCKS - 1
+    steps = [(u, first, HALF) for u in range(last_block) for first in (0, HALF)]
+    steps += [(last_block, sum(LAST_WIDTHS[:n]), width) for n, width in enumerate(LAST_WIDTHS)]
+
     with ExitStack() as ctx:
         held = ctx.enter_context(tc.tile_pool(name="held", bufs=1))
         ring = ctx.enter_context(tc.tile_pool(name="ring", bufs=2))
         psum = ctx.enter_context(tc.psum_pool(name="psum", bufs=1))
 
-        steps = [(0, 0, 512), (0, 512, 512), (1, 0, 512), (1, 512, 512), (2, 0, 512), (2, 512, 512), (3, 0, 256), (3, 256, 256), (3, 512, 256), (3, 768, 128), (3, 896, 128)]
-        fields = steps
-
         table_scales = held.tile([P, T], U8, name="table_scales")
         nc.gpsimd.memset(table_scales[:].bitcast(I32), 0)
-        offs_sb = held.tile([P, S // 16], U16, name="offs_sb")
+        offs_sb = held.tile([P, S // LIST_ROWS], U16, name="offs_sb")
         nc.sync.dma_start(offs_sb[:], offs)
-        unit_first = held.tile([P, 1], F32, name="unit_first")
-        nc.scalar.dma_start(unit_first[:], unit[:P, :])
-        for r in range(4):
-            queue = nc.scalar if r % 2 else nc.sync
-            queue.dma_start(table_scales[r:P:32, :].bitcast(I32), x_scales[0].bitcast(I32)[r:16:4, :])
-        table_words = held.tile([P, T], U32, name="table_words")
-        nc.sync.dma_start(
-            table_words[:].bitcast(I32), x_words[0].rearrange("p n t -> p (n t)").bitcast(I32)
-        )
+        scale_rows = x_scales[0].bitcast(I32)
+        for r in range(SCALE_ROWS):
+            nc.sync.dma_start(table_scales[r:P:QUADRANT, :].bitcast(I32), scale_rows[r::SCALE_ROWS, :])
+
         w1_rows = w1.rearrange("(p j) c -> p j c", j=PACK)
         w1_raw = [held.tile([P, PACK, P], F32, name=f"w1_raw{u}") for u in range(BLOCKS)]
-        nc.scalar.dma_start(w1_raw[0][:], w1_rows[:, :, :P])
-        lists = {name: held.tile([P, U // 16], U16, name=f"list_{name}") for name in "abc"}
-        nc.sync.dma_start(lists["c"][:], vc)
-        nc.sync.dma_start(lists["a"][:], va)
-        unit_rest = held.tile([P, BLOCKS - 1], F32, name="unit_rest")
-        units = [unit_first[:]] + [unit_rest[:, u : u + 1] for u in range(BLOCKS - 1)]
-        w2_raw = held.tile([P, PACK, N], F32, name="w2_raw")
-        weights = {}
-
-        def load_weights(u, first, width):
-            for name, src in (("a", wa), ("b", wb)):
-                loaded = held.tile([P, width], F32, name=f"w{name}{u}_{first}")
-                nc.sync.dma_start(loaded[:], src[u * P : (u + 1) * P, first : first + width])
-                for i, (block, start, size) in enumerate(steps):
-                    if block == u and first <= start < first + width:
-                        weights[i, name] = loaded[:, start - first : start - first + size]
 
         def load_w1(u):
             nc.sync.dma_start(w1_raw[u][:], w1_rows[:, :, u * P : (u + 1) * P])
 
-        def load_unit():
-            with nc.allow_non_contiguous_dma(reason="one factor a partition"):
-                nc.sync.dma_start(unit_rest[:], unit[P:, :].rearrange("(u p) o -> p (u o)", p=P))
+        weights = {}
 
-        def load_w2():
-            nc.sync.dma_start(w2_raw[:], w2.rearrange("(p j) m -> p j m", j=PACK))
+        def load_weights(u, first, width):
+            for corner, src in (("a", wa), ("b", wb)):
+                loaded = held.tile([P, width], F32, name=f"w{corner}{u}_{first}")
+                nc.sync.dma_start(loaded[:], src[u * P : (u + 1) * P, first : first + width])
+                for i, (block, start, size) in enumerate(steps):
+                    if block == u and first <= start < first + width:
+                        weights[i, corner] = loaded[:, start - first : start - first + size]
 
+        load_w1(0)
+        table_words = held.tile([P, T], U32, name="table_words")
+        nc.sync.dma_start(
+            table_words[:].bitcast(I32), x_words[0].rearrange("p n t -> p (n t)").bitcast(I32)
+        )
+        unit_first = held.tile([P, 1], F32, name="unit_first")
+        nc.sync.dma_start(unit_first[:], unit[:P, :])
+        lists = {corner: held.tile([P, U // LIST_ROWS], U16, name=f"list_{corner}") for corner in "abc"}
+        nc.sync.dma_start(lists["c"][:], vc)
+        nc.sync.dma_start(lists["a"][:], va)
         load_w1(1)
         load_weights(0, 0, HALF)
         nc.sync.dma_start(lists["b"][:], vb)
-        load_unit()
+        unit_rest = held.tile([P, BLOCKS - 1], F32, name="unit_rest")
+        with nc.allow_non_contiguous_dma(reason="one factor a partition and block"):
+            nc.sync.dma_start(unit_rest[:], unit[P:, :].rearrange("(u p) o -> p (u o)", p=P))
+        units = [unit_first[:]] + [unit_rest[:, u : u + 1] for u in range(BLOCKS - 1)]
         load_weights(0, HALF, HALF)
-        load_w1(2)
-        load_w1(3)
+        for u in range(2, BLOCKS):
+            load_w1(u)
         load_weights(1, 0, U)
-        load_w2()
-        load_weights(2, 0, U)
-        load_weights(3, 0, U)
+        w2_raw = held.tile([P, PACK, N], F32, name="w2_raw")
+        nc.sync.dma_start(w2_raw[:], w2.rearrange("(p j) m -> p j m", j=PACK))
+        for u in range(2, BLOCKS):
+            load_weights(u, 0, U)
 
+        windows = [held.tile([P, S + SPARE], F32, name=f"window{u}") for u in range(BLOCKS)]
+        for window in windows:
+            nc.gpsimd.memset(window[:, S:], 0.0)
         ident = held.tile([P, P], F32, name="ident")
-        windows = [held.tile([P, WINDOW], F32, name=f"window{u}") for u in range(BLOCKS)]
-        for u in range(BLOCKS):
-            nc.gpsimd.memset(windows[u][:, S:], 0.0)
         make_identity(nc, ident[:])
 
-        def quantise_weight(raw, name, on_scalar):
+        def round_on_scalar(dst, src):
+            nc.scalar.activation(dst, src, COPY)
+
+        def quantise_weight(raw, name, round_copy):
             grouped = held.tile([P, P, PACK], BF16, name=f"{name}_bf", align_bytes=64)
-            if on_scalar:
-                nc.scalar.activation(grouped[:], raw[:].rearrange("p j c -> p c j"), COPY)
-            else:
-                nc.vector.tensor_copy(grouped[:], raw[:].rearrange("p j c -> p c j"))
+            round_copy(grouped[:], raw[:].rearrange("p j c -> p c j"))
             codes = held.tile([P, P], U32, name=f"{name}_codes", align_bytes=64)
             scales = held.tile([P, P], U8, name=f"{name}_scales", align_bytes=64)
             nc.vector.quantize_mx(
@@ -115,88 +113,98 @@ def tile_picked_ybaryin_lin_p_kernel(
         x_codes = held.tile([P, S], U32, name="x_codes", align_bytes=64)
         x_bytes = held.tile([P, S], U8, name="x_bytes", align_bytes=64)
         nc.vector.tensor_copy(x_bytes[:], table_scales[:].indirect(offs_sb[:]))
-        x_width = S // X_PARTS
-        for at in range(0, S, x_width):
+        x_half = S // 2
+        for at in (0, x_half):
             nc.vector.tensor_copy(
-                x_codes[:, at : at + x_width],
-                table_words[:].indirect(offs_sb[:, at // 16 : (at + x_width) // 16]),
+                x_codes[:, at : at + x_half],
+                table_words[:].indirect(offs_sb[:, at // LIST_ROWS : (at + x_half) // LIST_ROWS]),
             )
 
-        def coarse_block(u):
-            codes, scales = quantise_weight(w1_raw[u], f"w1_{u}", u in (0,))
-            width = x_width if u == 0 else S
+        def make_window(u):
+            round_copy = round_on_scalar if u == 0 else nc.vector.tensor_copy
+            codes, scales = quantise_weight(w1_raw[u], f"w1_{u}", round_copy)
+            width = x_half if u == 0 else S
             for at in range(0, S, width):
                 y = psum.tile([P, width], F32, name="y", tag="mx", bufs=2)
                 nc.tensor.matmul_mx(
-                    out=y[:], lhsT=codes[:].bitcast(FP8X4), lhsT_scale=scales[:],
-                    rhs=x_codes[:, at : at + width].bitcast(FP8X4), rhs_scale=x_bytes[:, at : at + width],
-                    start=True, stop=True,
+                    out=y[:],
+                    lhsT=codes[:].bitcast(FP8X4),
+                    lhsT_scale=scales[:],
+                    rhs=x_codes[:, at : at + width].bitcast(FP8X4),
+                    rhs_scale=x_bytes[:, at : at + width],
+                    start=True,
+                    stop=True,
                 )
                 nc.scalar.activation(windows[u][:, at : at + width], y[:], COPY, scale=units[u])
 
-        def corners(name, u, first, width):
-            return windows[u][:].indirect(lists[name][:, first // 16 : (first + width) // 16])
+        def looked_up(i, corner):
+            u, first, width = steps[i]
+            return windows[u][:].indirect(lists[corner][:, first // LIST_ROWS : (first + width) // LIST_ROWS])
 
-        fetched, minus_sum = {}, {}
+        fetched, minus_sum, sums = {}, {}, {}
 
-        def scalar_fetch(f):
-            u, first, width = steps[f]
-            for name in ("c",) if f in VECTOR_B else ("c", "b"):
-                fetched[f, name] = ring.tile([P, width], F32, name=f"fetched_{name}", bufs=2)
-                nc.scalar.activation(fetched[f, name][:], corners(name, u, first, width), COPY)
+        def fetch(i):
+            for corner in "c" if i == 0 else "cb":
+                fetched[i, corner] = ring.tile([P, steps[i][2]], F32, name=f"fetched_{corner}")
+                nc.scalar.activation(fetched[i, corner][:], looked_up(i, corner), COPY)
 
-        def add_weights(f):
-            minus_sum[f] = ring.tile([P, steps[f][2]], F32, name="minus_sum", bufs=2)
+        def add_weights(i):
+            minus_sum[i] = ring.tile([P, steps[i][2]], F32, name="minus_sum")
             nc.vector.scalar_tensor_tensor(
-                minus_sum[f][:], weights[f, "a"], -1.0, weights[f, "b"], ALU.mult, ALU.subtract
+                minus_sum[i][:], weights[i, "a"], -1.0, weights[i, "b"], ALU.mult, ALU.subtract
             )
 
-        sums = {}
+        def make_sums(i):
+            width = steps[i][2]
+            term = {corner: ring.tile([P, width], F32, name=f"term_{corner}") for corner in "abc"}
 
-        def terms(i):
-            u, first, width = steps[i]
-            f = i
-            cols = slice(0, width)
-            term = {name: ring.tile([P, width], F32, name=f"term_{name}") for name in "abc"}
-            nc.vector.tensor_tensor(term["a"][:], corners("a", u, first, width), weights[f, "a"], ALU.mult)
-            corner_b = corners("b", u, first, width) if f in VECTOR_B else fetched[f, "b"][:, cols]
-            order = "abc" if f in VECTOR_B else "acb"
-            for name in order[1:]:
-                if name == "b":
-                    nc.vector.tensor_tensor(term["b"][:], corner_b, weights[f, "b"], ALU.mult)
-                else:
-                    nc.vector.scalar_tensor_tensor(
-                        term["c"][:], minus_sum[f][:, cols], 1.0, fetched[f, "c"][:, cols], ALU.add, ALU.mult
-                    )
+            def term_b():
+                corner_b = looked_up(i, "b") if i == 0 else fetched[i, "b"][:]
+                nc.vector.tensor_tensor(term["b"][:], corner_b, weights[i, "b"], ALU.mult)
+
+            def term_c():
+                nc.vector.scalar_tensor_tensor(
+                    term["c"][:], minus_sum[i][:], 1.0, fetched[i, "c"][:], ALU.add, ALU.mult
+                )
+
+            order = "abc" if i == 0 else "acb"
+            nc.vector.tensor_tensor(term["a"][:], looked_up(i, "a"), weights[i, "a"], ALU.mult)
+            for corner in order[1:]:
+                {"b": term_b, "c": term_c}[corner]()
+
             chunks = width // P
             sums[i] = psum.tile([P, chunks, P], F32, name="sums", bufs=4)
-            for name in order:
+            for corner in order:
                 for c in range(chunks):
                     nc.tensor.matmul(
-                        sums[i][:, c, :], lhsT=term[name][:, c * P : (c + 1) * P], rhs=ident[:],
-                        start=(name == order[0] and c == 0), stop=(name == order[-1] and c == chunks - 1),
+                        sums[i][:, c, :],
+                        lhsT=term[corner][:, c * P : (c + 1) * P],
+                        rhs=ident[:],
+                        start=(corner == order[0] and c == 0),
+                        stop=(corner == order[-1] and c == chunks - 1),
                         is_transpose=True,
                     )
 
-        turned = held.tile([P, 2, U // P, P, 2], BF16, name="turned")
+        turned = held.tile([P, PAIRS, U // P, P, 2], BF16, name="turned")
         turned_words = turned[:].rearrange("r w c p e -> r (w c p e)").bitcast(F32)
+        words_a_block = P // PACK
 
         def round_sums(i):
             u, first, width = steps[i]
-            (nc.scalar.copy)(
-                turned[:, :, first // P : (first + width) // P, 32 * u : 32 * (u + 1), :],
-                sums[i][:].rearrange("r c (q w e) -> r w c q e", w=2, e=2),
+            nc.scalar.copy(
+                turned[:, :, first // P : (first + width) // P, words_a_block * u : words_a_block * (u + 1), :],
+                sums[i][:].rearrange("r c (q w e) -> r w c q e", w=PAIRS, e=2),
             )
 
-        def decode(first, width, copy_words, copy_out):
-            grouped = ring.tile([P, width, PACK], BF16, name="hid_bf", align_bytes=64)
-            back = psum.tile([P, 2, width], F32, name="back", bufs=2)
-            for w in range(2):
+        def decode(first, width, move_words):
+            back = psum.tile([P, PAIRS, width], F32, name="back", bufs=2)
+            for w in range(PAIRS):
                 for c in range(width // P):
                     at = w * U + first + c * P
                     nc.tensor.transpose(back[:, w, c * P : (c + 1) * P], turned_words[:, at : at + P], ident[:])
-            copy_words(
-                grouped[:].rearrange("p r j -> p (r j)").bitcast(F32).rearrange("p (r w) -> p r w", w=2),
+            grouped = ring.tile([P, width, PACK], BF16, name="hid_bf", align_bytes=64)
+            move_words(
+                grouped[:].rearrange("p r j -> p (r j)").bitcast(F32).rearrange("p (r w) -> p r w", w=PAIRS),
                 back[:].rearrange("p w r -> p r w"),
             )
             codes = ring.tile([P, width], U32, name="hid_codes", align_bytes=64)
@@ -206,41 +214,36 @@ def tile_picked_ybaryin_lin_p_kernel(
             )
             result = psum.tile([P, width], F32, name="result", tag="mx", bufs=2)
             nc.tensor.matmul_mx(
-                out=result[:], lhsT=w2_codes[:].bitcast(FP8X4), lhsT_scale=w2_scales[:],
-                rhs=codes[:].bitcast(FP8X4), rhs_scale=scales[:], start=True, stop=True,
+                out=result[:],
+                lhsT=w2_codes[:].bitcast(FP8X4),
+                lhsT_scale=w2_scales[:],
+                rhs=codes[:].bitcast(FP8X4),
+                rhs_scale=scales[:],
+                start=True,
+                stop=True,
             )
             staged = held.tile([P, width], F32, name=f"staged{first}")
-            copy_out(staged[:], result[:])
+            nc.scalar.copy(staged[:], result[:])
             nc.sync.dma_start(out[:, first : first + width], staged[:])
 
         def finish(i):
             round_sums(i)
             u, first, width = steps[i]
-            last = i == len(steps) - 1
-            if u == BLOCKS - 1:
-                for at in range(first, first + width, PIECE):
-                    decode(
-                        at,
-                        min(PIECE, first + width - at),
-                        nc.vector.tensor_copy if last else nc.scalar.copy,
-                        nc.vector.tensor_copy if False else nc.scalar.copy,
-                    )
+            if u == last_block:
+                decode(first, width, nc.vector.tensor_copy if i == len(steps) - 1 else nc.scalar.copy)
 
-        made = {0}
-        coarse_block(0)
-        scalar_fetch(0)
+        make_window(0)
+        fetch(0)
         add_weights(0)
         for i in range(len(steps)):
-            ahead = steps[min(i + 2, len(steps) - 1)][0]
-            if ahead not in made:
-                made.add(ahead)
-                coarse_block(ahead)
-            if i == 4:
-                w2_codes, w2_scales = quantise_weight(w2_raw, "w2", True)
-            if i + 1 < len(fields):
-                scalar_fetch(i + 1)
-            terms(i)
-            if i + 1 < len(fields):
+            if i + 2 < len(steps) and steps[i + 2][1] == 0:
+                make_window(steps[i + 2][0])
+            if i + 1 < len(steps) and steps[i + 1] == (BLOCKS // 2, 0, HALF):
+                w2_codes, w2_scales = quantise_weight(w2_raw, "w2", round_on_scalar)
+            if i + 1 < len(steps):
+                fetch(i + 1)
+            make_sums(i)
+            if i + 1 < len(steps):
                 add_weights(i + 1)
             if i > 0:
                 finish(i - 1)

@@ -22,7 +22,8 @@ QUADRANT = 32
 SCALE_ROWS = 4
 BLOCKS = H // P
 HALF = U // 2
-LAST_WIDTHS = (256, 256, 256, 128, 128)
+BANK = 512
+WIDTHS = ((HALF, HALF), (U,), (U,), (256, 256, 256, 128, 128))
 SPARE = 16
 
 FLOPS = 2 * K * H * S + 2 * H * N * U
@@ -33,8 +34,8 @@ def tile_picked_ybaryin_lin_p_kernel(
 ):
     nc = tc.nc
     last_block = BLOCKS - 1
-    steps = [(u, first, HALF) for u in range(last_block) for first in (0, HALF)]
-    steps += [(last_block, sum(LAST_WIDTHS[:n]), width) for n, width in enumerate(LAST_WIDTHS)]
+    steps = [(u, sum(WIDTHS[u][:n]), width) for u in range(BLOCKS) for n, width in enumerate(WIDTHS[u])]
+    b_on_vector = [i == 0 or (u == last_block and first >= HALF) for i, (u, first, width) in enumerate(steps)]
 
     with ExitStack() as ctx:
         held = ctx.enter_context(tc.tile_pool(name="held", bufs=1))
@@ -45,15 +46,23 @@ def tile_picked_ybaryin_lin_p_kernel(
         nc.gpsimd.memset(table_scales[:].bitcast(I32), 0)
         offs_sb = held.tile([P, S // LIST_ROWS], U16, name="offs_sb")
         nc.sync.dma_start(offs_sb[:], offs)
+        unit_first = held.tile([P, 1], F32, name="unit_first")
+        nc.scalar.dma_start(unit_first[:], unit[:P, :])
         scale_rows = x_scales[0].bitcast(I32)
         for r in range(SCALE_ROWS):
-            nc.sync.dma_start(table_scales[r:P:QUADRANT, :].bitcast(I32), scale_rows[r::SCALE_ROWS, :])
+            queue = nc.scalar if r % 2 else nc.sync
+            queue.dma_start(table_scales[r:P:QUADRANT, :].bitcast(I32), scale_rows[r::SCALE_ROWS, :])
+        table_words = held.tile([P, T], U32, name="table_words")
+        nc.sync.dma_start(
+            table_words[:].bitcast(I32), x_words[0].rearrange("p n t -> p (n t)").bitcast(I32)
+        )
 
         w1_rows = w1.rearrange("(p j) c -> p j c", j=PACK)
         w1_raw = [held.tile([P, PACK, P], F32, name=f"w1_raw{u}") for u in range(BLOCKS)]
 
         def load_w1(u):
-            nc.sync.dma_start(w1_raw[u][:], w1_rows[:, :, u * P : (u + 1) * P])
+            queue = nc.scalar if u == 0 else nc.sync
+            queue.dma_start(w1_raw[u][:], w1_rows[:, :, u * P : (u + 1) * P])
 
         weights = {}
 
@@ -66,12 +75,6 @@ def tile_picked_ybaryin_lin_p_kernel(
                         weights[i, corner] = loaded[:, start - first : start - first + size]
 
         load_w1(0)
-        table_words = held.tile([P, T], U32, name="table_words")
-        nc.sync.dma_start(
-            table_words[:].bitcast(I32), x_words[0].rearrange("p n t -> p (n t)").bitcast(I32)
-        )
-        unit_first = held.tile([P, 1], F32, name="unit_first")
-        nc.sync.dma_start(unit_first[:], unit[:P, :])
         lists = {corner: held.tile([P, U // LIST_ROWS], U16, name=f"list_{corner}") for corner in "abc"}
         nc.sync.dma_start(lists["c"][:], vc)
         nc.sync.dma_start(lists["a"][:], va)
@@ -91,7 +94,9 @@ def tile_picked_ybaryin_lin_p_kernel(
         for u in range(2, BLOCKS):
             load_weights(u, 0, U)
 
-        windows = [held.tile([P, S + SPARE], F32, name=f"window{u}") for u in range(BLOCKS)]
+        windows = [
+            held.tile([P, max(S, *WIDTHS[u]) + SPARE], F32, name=f"window{u}") for u in range(BLOCKS)
+        ]
         for window in windows:
             nc.gpsimd.memset(window[:, S:], 0.0)
         ident = held.tile([P, P], F32, name="ident")
@@ -144,7 +149,7 @@ def tile_picked_ybaryin_lin_p_kernel(
         fetched, minus_sum, sums = {}, {}, {}
 
         def fetch(i):
-            for corner in "c" if i == 0 else "cb":
+            for corner in "c" if b_on_vector[i] else "cb":
                 fetched[i, corner] = ring.tile([P, steps[i][2]], F32, name=f"fetched_{corner}")
                 nc.scalar.activation(fetched[i, corner][:], looked_up(i, corner), COPY)
 
@@ -159,7 +164,7 @@ def tile_picked_ybaryin_lin_p_kernel(
             term = {corner: ring.tile([P, width], F32, name=f"term_{corner}") for corner in "abc"}
 
             def term_b():
-                corner_b = looked_up(i, "b") if i == 0 else fetched[i, "b"][:]
+                corner_b = looked_up(i, "b") if b_on_vector[i] else fetched[i, "b"][:]
                 nc.vector.tensor_tensor(term["b"][:], corner_b, weights[i, "b"], ALU.mult)
 
             def term_c():
@@ -167,23 +172,26 @@ def tile_picked_ybaryin_lin_p_kernel(
                     term["c"][:], minus_sum[i][:], 1.0, fetched[i, "c"][:], ALU.add, ALU.mult
                 )
 
-            order = "abc" if i == 0 else "acb"
+            order = "abc" if b_on_vector[i] else "acb"
             nc.vector.tensor_tensor(term["a"][:], looked_up(i, "a"), weights[i, "a"], ALU.mult)
             for corner in order[1:]:
                 {"b": term_b, "c": term_c}[corner]()
 
-            chunks = width // P
-            sums[i] = psum.tile([P, chunks, P], F32, name="sums", bufs=4)
+            chunks = min(width, BANK) // P
+            sums[i] = [
+                (at, psum.tile([P, chunks, P], F32, name="sums", bufs=4)) for at in range(0, width, BANK)
+            ]
             for corner in order:
-                for c in range(chunks):
-                    nc.tensor.matmul(
-                        sums[i][:, c, :],
-                        lhsT=term[corner][:, c * P : (c + 1) * P],
-                        rhs=ident[:],
-                        start=(corner == order[0] and c == 0),
-                        stop=(corner == order[-1] and c == chunks - 1),
-                        is_transpose=True,
-                    )
+                for at, bank in sums[i]:
+                    for c in range(chunks):
+                        nc.tensor.matmul(
+                            bank[:, c, :],
+                            lhsT=term[corner][:, at + c * P : at + (c + 1) * P],
+                            rhs=ident[:],
+                            start=(corner == order[0] and c == 0),
+                            stop=(corner == order[-1] and c == chunks - 1),
+                            is_transpose=True,
+                        )
 
         turned = held.tile([P, PAIRS, U // P, P, 2], BF16, name="turned")
         turned_words = turned[:].rearrange("r w c p e -> r (w c p e)").bitcast(F32)
@@ -191,10 +199,13 @@ def tile_picked_ybaryin_lin_p_kernel(
 
         def round_sums(i):
             u, first, width = steps[i]
-            nc.scalar.copy(
-                turned[:, :, first // P : (first + width) // P, words_a_block * u : words_a_block * (u + 1), :],
-                sums[i][:].rearrange("r c (q w e) -> r w c q e", w=PAIRS, e=2),
-            )
+            own_words = slice(words_a_block * u, words_a_block * (u + 1))
+            for at, bank in sums[i]:
+                chunk = (first + at) // P
+                nc.scalar.copy(
+                    turned[:, :, chunk : chunk + min(width, BANK) // P, own_words, :],
+                    bank[:].rearrange("r c (q w e) -> r w c q e", w=PAIRS, e=2),
+                )
 
         def decode(first, width, move_words):
             back = psum.tile([P, PAIRS, width], F32, name="back", bufs=2)
@@ -238,7 +249,7 @@ def tile_picked_ybaryin_lin_p_kernel(
         for i in range(len(steps)):
             if i + 2 < len(steps) and steps[i + 2][1] == 0:
                 make_window(steps[i + 2][0])
-            if i + 1 < len(steps) and steps[i + 1] == (BLOCKS // 2, 0, HALF):
+            if steps[i][:2] == (last_block, 0):
                 w2_codes, w2_scales = quantise_weight(w2_raw, "w2", round_on_scalar)
             if i + 1 < len(steps):
                 fetch(i + 1)

from contextlib import ExitStack

import concourse.mybir as mybir
from concourse.masks import make_identity

F32 = mybir.dt.float32
BF16 = mybir.dt.bfloat16
I32 = mybir.dt.int32
U32 = mybir.dt.uint32
U16 = mybir.dt.uint16
U8 = mybir.dt.uint8
FP8X4 = mybir.dt.float8_e4m3fn_x4
ALU = mybir.AluOpType
COPY = mybir.ActivationFunctionType.Copy

K, T, S, N, H, U = 512, 1024, 512, 128, 512, 1024
P = 128
PACK = 4
PAIRS = PACK // 2
LIST_ROWS = 16
QUADRANT = 32
SCALE_ROWS = 4
BLOCKS = H // P
HALF = U // 2
BANK = 512
WIDTHS = ((HALF, HALF), (U,), (U,), (256, 256, 256, 128, 128))
SPARE = 16

FLOPS = 2 * K * H * S + 2 * H * N * U


def tile_picked_ybaryin_lin_p_kernel(
    tc, x_words, x_scales, w1, wa, wb, unit, w2, offs, va, vb, vc, out
):
    nc = tc.nc
    last_block = BLOCKS - 1
    steps = [(u, sum(WIDTHS[u][:n]), width) for u in range(BLOCKS) for n, width in enumerate(WIDTHS[u])]
    b_on_vector = [i == 0 or (u == last_block and first >= HALF) for i, (u, first, width) in enumerate(steps)]

    with ExitStack() as ctx:
        held = ctx.enter_context(tc.tile_pool(name="held", bufs=1))
        ring = ctx.enter_context(tc.tile_pool(name="ring", bufs=2))
        psum = ctx.enter_context(tc.psum_pool(name="psum", bufs=1))

        table_scales = held.tile([P, T], U8, name="table_scales")
        nc.gpsimd.memset(table_scales[:].bitcast(I32), 0)
        offs_sb = held.tile([P, S // LIST_ROWS], U16, name="offs_sb")
        nc.sync.dma_start(offs_sb[:], offs)
        unit_first = held.tile([P, 1], F32, name="unit_first")
        nc.scalar.dma_start(unit_first[:], unit[:P, :])
        scale_rows = x_scales[0].bitcast(I32)
        for r in range(SCALE_ROWS):
            queue = nc.scalar if r % 2 else nc.sync
            queue.dma_start(table_scales[r:P:QUADRANT, :].bitcast(I32), scale_rows[r::SCALE_ROWS, :])
        table_words = held.tile([P, T], U32, name="table_words")
        nc.sync.dma_start(
            table_words[:].bitcast(I32), x_words[0].rearrange("p n t -> p (n t)").bitcast(I32)
        )

        w1_rows = w1.rearrange("(p j) c -> p j c", j=PACK)
        w1_raw = [held.tile([P, PACK, P], F32, name=f"w1_raw{u}") for u in range(BLOCKS)]

        def load_w1(u):
            queue = nc.scalar if u == 0 else nc.sync
            queue.dma_start(w1_raw[u][:], w1_rows[:, :, u * P : (u + 1) * P])

        weights = {}

        def load_weights(u, first, width):
            for corner, src in (("a", wa), ("b", wb)):
                loaded = held.tile([P, width], F32, name=f"w{corner}{u}_{first}")
                nc.sync.dma_start(loaded[:], src[u * P : (u + 1) * P, first : first + width])
                for i, (block, start, size) in enumerate(steps):
                    if block == u and first <= start < first + width:
                        weights[i, corner] = loaded[:, start - first : start - first + size]

        load_w1(0)
        lists = {corner: held.tile([P, U // LIST_ROWS], U16, name=f"list_{corner}") for corner in "abc"}
        nc.sync.dma_start(lists["c"][:], vc)
        nc.sync.dma_start(lists["a"][:], va)
        load_w1(1)
        load_weights(0, 0, HALF)
        nc.sync.dma_start(lists["b"][:], vb)
        unit_rest = held.tile([P, BLOCKS - 1], F32, name="unit_rest")
        with nc.allow_non_contiguous_dma(reason="one factor a partition and block"):
            nc.sync.dma_start(unit_rest[:], unit[P:, :].rearrange("(u p) o -> p (u o)", p=P))
        units = [unit_first[:]] + [unit_rest[:, u : u + 1] for u in range(BLOCKS - 1)]
        load_weights(0, HALF, HALF)
        for u in range(2, BLOCKS):
            load_w1(u)
        load_weights(1, 0, U)
        w2_raw = held.tile([P, PACK, N], F32, name="w2_raw")
        nc.sync.dma_start(w2_raw[:], w2.rearrange("(p j) m -> p j m", j=PACK))
        for u in range(2, BLOCKS):
            load_weights(u, 0, U)

        windows = [
            held.tile([P, max(S, *WIDTHS[u]) + SPARE], F32, name=f"window{u}") for u in range(BLOCKS)
        ]
        for window in windows:
            nc.gpsimd.memset(window[:, S:], 0.0)
        ident = held.tile([P, P], F32, name="ident")
        make_identity(nc, ident[:])

        def round_on_scalar(dst, src):
            nc.scalar.activation(dst, src, COPY)

        def quantise_weight(raw, name, round_copy):
            grouped = held.tile([P, P, PACK], BF16, name=f"{name}_bf", align_bytes=64)
            round_copy(grouped[:], raw[:].rearrange("p j c -> p c j"))
            codes = held.tile([P, P], U32, name=f"{name}_codes", align_bytes=64)
            scales = held.tile([P, P], U8, name=f"{name}_scales", align_bytes=64)
            nc.vector.quantize_mx(
                out=codes[:].bitcast(FP8X4), scales=scales[:], in_=grouped[:].rearrange("p c j -> p (c j)")
            )
            return codes, scales

        x_codes = held.tile([P, S], U32, name="x_codes", align_bytes=64)
        x_bytes = held.tile([P, S], U8, name="x_bytes", align_bytes=64)
        nc.vector.tensor_copy(x_bytes[:], table_scales[:].indirect(offs_sb[:]))
        x_half = S // 2
        for at in (0, x_half):
            nc.vector.tensor_copy(
                x_codes[:, at : at + x_half],
                table_words[:].indirect(offs_sb[:, at // LIST_ROWS : (at + x_half) // LIST_ROWS]),
            )

        def make_window(u):
            round_copy = round_on_scalar if u == 0 else nc.vector.tensor_copy
            codes, scales = quantise_weight(w1_raw[u], f"w1_{u}", round_copy)
            width = x_half if u == 0 else S
            for at in range(0, S, width):
                y = psum.tile([P, width], F32, name="y", tag="mx", bufs=2)
                nc.tensor.matmul_mx(
                    out=y[:],
                    lhsT=codes[:].bitcast(FP8X4),
                    lhsT_scale=scales[:],
                    rhs=x_codes[:, at : at + width].bitcast(FP8X4),
                    rhs_scale=x_bytes[:, at : at + width],
                    start=True,
                    stop=True,
                )
                nc.scalar.activation(windows[u][:, at : at + width], y[:], COPY, scale=units[u])

        def looked_up(i, corner):
            u, first, width = steps[i]
            return windows[u][:].indirect(lists[corner][:, first // LIST_ROWS : (first + width) // LIST_ROWS])

        fetched, minus_sum, sums = {}, {}, {}

        def fetch(i):
            for corner in "c" if b_on_vector[i] else "cb":
                fetched[i, corner] = ring.tile([P, steps[i][2]], F32, name=f"fetched_{corner}")
                nc.scalar.activation(fetched[i, corner][:], looked_up(i, corner), COPY)

        def add_weights(i):
            minus_sum[i] = ring.tile([P, steps[i][2]], F32, name="minus_sum")
            nc.vector.scalar_tensor_tensor(
                minus_sum[i][:], weights[i, "a"], -1.0, weights[i, "b"], ALU.mult, ALU.subtract
            )

        def make_sums(i):
            width = steps[i][2]
            term = {corner: ring.tile([P, width], F32, name=f"term_{corner}") for corner in "abc"}

            def term_b():
                corner_b = looked_up(i, "b") if b_on_vector[i] else fetched[i, "b"][:]
                nc.vector.tensor_tensor(term["b"][:], corner_b, weights[i, "b"], ALU.mult)

            def term_c():
                nc.vector.scalar_tensor_tensor(
                    term["c"][:], minus_sum[i][:], 1.0, fetched[i, "c"][:], ALU.add, ALU.mult
                )

            order = "abc" if b_on_vector[i] else "acb"
            nc.vector.tensor_tensor(term["a"][:], looked_up(i, "a"), weights[i, "a"], ALU.mult)
            for corner in order[1:]:
                {"b": term_b, "c": term_c}[corner]()

            chunks = min(width, BANK) // P
            sums[i] = [
                (at, psum.tile([P, chunks, P], F32, name="sums", bufs=4)) for at in range(0, width, BANK)
            ]
            for corner in order:
                for at, bank in sums[i]:
                    for c in range(chunks):
                        nc.tensor.matmul(
                            bank[:, c, :],
                            lhsT=term[corner][:, at + c * P : at + (c + 1) * P],
                            rhs=ident[:],
                            start=(corner == order[0] and c == 0),
                            stop=(corner == order[-1] and c == chunks - 1),
                            is_transpose=True,
                        )

        turned = held.tile([P, PAIRS, U // P, P, 2], BF16, name="turned")
        turned_words = turned[:].rearrange("r w c p e -> r (w c p e)").bitcast(F32)
        words_a_block = P // PACK

        def round_sums(i):
            u, first, width = steps[i]
            own_words = slice(words_a_block * u, words_a_block * (u + 1))
            for at, bank in sums[i]:
                chunk = (first + at) // P
                nc.scalar.copy(
                    turned[:, :, chunk : chunk + min(width, BANK) // P, own_words, :],
                    bank[:].rearrange("r c (q w e) -> r w c q e", w=PAIRS, e=2),
                )

        def decode(first, width, move_words):
            back = psum.tile([P, PAIRS, width], F32, name="back", bufs=2)
            for w in range(PAIRS):
                for c in range(width // P):
                    at = w * U + first + c * P
                    nc.tensor.transpose(back[:, w, c * P : (c + 1) * P], turned_words[:, at : at + P], ident[:])
            grouped = ring.tile([P, width, PACK], BF16, name="hid_bf", align_bytes=64)
            move_words(
                grouped[:].rearrange("p r j -> p (r j)").bitcast(F32).rearrange("p (r w) -> p r w", w=PAIRS),
                back[:].rearrange("p w r -> p r w"),
            )
            codes = ring.tile([P, width], U32, name="hid_codes", align_bytes=64)
            scales = ring.tile([P, width], U8, name="hid_scales", align_bytes=64)
            nc.vector.quantize_mx(
                out=codes[:].bitcast(FP8X4), scales=scales[:], in_=grouped[:].rearrange("p r j -> p (r j)")
            )
            result = psum.tile([P, width], F32, name="result", tag="mx", bufs=2)
            nc.tensor.matmul_mx(
                out=result[:],
                lhsT=w2_codes[:].bitcast(FP8X4),
                lhsT_scale=w2_scales[:],
                rhs=codes[:].bitcast(FP8X4),
                rhs_scale=scales[:],
                start=True,
                stop=True,
            )
            staged = held.tile([P, width], F32, name=f"staged{first}")
            nc.scalar.copy(staged[:], result[:])
            nc.sync.dma_start(out[:, first : first + width], staged[:])

        def finish(i):
            round_sums(i)
            u, first, width = steps[i]
            if u == last_block:
                decode(first, width, nc.vector.tensor_copy if i == len(steps) - 1 else nc.scalar.copy)

        make_window(0)
        fetch(0)
        add_weights(0)
        for i in range(len(steps)):
            if i + 2 < len(steps) and steps[i + 2][1] == 0:
                make_window(steps[i + 2][0])
            if steps[i][:2] == (last_block, 0):
                w2_codes, w2_scales = quantise_weight(w2_raw, "w2", round_on_scalar)
            if i + 1 < len(steps):
                fetch(i + 1)
            make_sums(i)
            if i + 1 < len(steps):
                add_weights(i + 1)
            if i > 0:
                finish(i - 1)
        finish(len(steps) - 1)
